import numpy as np
CORES = [0,4,8,12,16,20,24,28]
N = 8
def setup_inputs(rng):
    return {"x": rng.standard_normal((N, 128, 1024), dtype=np.float32)}
def reference(x):
    b = 1024 // N
    blocks = x.reshape(N, 128, N, b)
    return {"y": np.ascontiguousarray(blocks.transpose(2, 1, 0, 3)).reshape(N, 128, 1024)}

from concourse.bass import DstId, RemoteDMATransfer

B = 128

SCRATCH = {
    "xs": ("sbuf", [128, 1024], "float32"),
    "land": ("sbuf", [128, 1024], "float32"),
    "hb": ("sbuf", [128, 256], "float32"),
}
SEMAPHORES = ["ld_relay", "ld_direct", "sent", "arr_h", "arr_p", "arr_w", "arr_m", "arr_t", "stored"]


def _blk(j):
    return slice(j * B, (j + 1) * B)


def _pair(ch):
    return slice(ch * 2 * B, (ch + 1) * 2 * B)


def _xfer(topo, dst_core, mask, sem, src, dst):
    rid, pid, _se = topo.addr(dst_core)
    return RemoteDMATransfer(dst_ids=[DstId(rid=rid, pnc=pid)], dma_engine_mask=mask, remote_sem=sem,
                             src=src, dst=dst)


def _helper(g, core, T, topo, src_rank, dst_chip, sem):
    S = T.sem
    g.wait_ge(S.arr_h, 8)
    g.remote_dma_fused(
        [_xfer(topo, T.cores[2 * dst_chip + i], 0x000F << (4 * i), sem,
               T.hb[:, _blk(i)], T.land[:, _blk(src_rank)]) for i in range(2)],
        local_sem=S.sent)
    g.wait_ge(S.sent, 8)


def rank_program(g, core, T, topo):
    S = T.sem
    rank = T.rank_of(core)
    if rank is None:
        k = core % 4
        if k < 2:
            return
        src = T.rank_of(core - k)
        ch = src // 2
        if k == 2:
            _helper(g, core, T, topo, src, ch ^ 1, S.arr_m)
        else:
            _helper(g, core, T, topo, src, ch ^ 3, S.arr_t)
        return

    ch = rank // 2
    mate, far, plane, peer = ch ^ 1, ch ^ 3, ch ^ 2, rank ^ 1
    sy, sc = g.sync, g.scalar

    sy.dma_start(T.xs[:, _pair(far)], T.x[:, _pair(far)]).then_inc(S.ld_relay, 16)
    sc.dma_start(T.xs[:, _pair(mate)], T.x[:, _pair(mate)]).then_inc(S.ld_relay, 16)
    sy.dma_start(T.xs[:, _pair(plane)], T.x[:, _pair(plane)]).then_inc(S.ld_direct, 16)
    sc.dma_start(T.xs[:, _blk(peer)], T.x[:, _blk(peer)]).then_inc(S.ld_direct, 16)

    g.wait_ge(S.ld_relay, 32)
    g.remote_dma_fused(
        [_xfer(topo, core + 3, 0x00FF, S.arr_h, T.xs[:, _pair(far)], T.hb[:, :]),
         _xfer(topo, core + 2, 0xFF00, S.arr_h, T.xs[:, _pair(mate)], T.hb[:, :])],
        local_sem=S.sent)
    g.wait_ge(S.ld_direct, 32)
    g.remote_dma_fused(
        [_xfer(topo, T.cores[2 * plane + i], 0x000F << (4 * i), S.arr_w,
               T.xs[:, _blk(2 * plane + i)], T.land[:, _blk(rank)]) for i in range(2)]
        + [_xfer(topo, T.cores[peer], 0xFF00, S.arr_p, T.xs[:, _blk(peer)], T.land[:, _blk(rank)])],
        local_sem=S.sent)

    sc.wait_ge(S.arr_p, 8)
    sc.dma_start(T.y[:, _blk(peer)], T.land[:, _blk(peer)]).then_inc(S.stored, 16)
    sc.dma_start(T.y[:, _blk(rank)], T.x[:, _blk(rank)]).then_inc(S.stored, 16)
    sy.wait_ge(S.arr_w, 8)
    sy.dma_start(T.y[:, _pair(plane)], T.land[:, _pair(plane)]).then_inc(S.stored, 16)
    sy.wait_ge(S.arr_m, 8)
    sy.dma_start(T.y[:, _pair(mate)], T.land[:, _pair(mate)]).then_inc(S.stored, 16)
    sc.wait_ge(S.arr_t, 8)
    sc.dma_start(T.y[:, _pair(far)], T.land[:, _pair(far)]).then_inc(S.stored, 16)

    g.wait_ge(S.sent, 32)
    g.wait_ge(S.stored, 80)
